import numpy as np
import ml_dtypes


def mxq(x, axis, fmt="e4m3"):
    dtype, down = {"e4m3": (ml_dtypes.float8_e4m3fn, 7), "e5m2": (ml_dtypes.float8_e5m2, 14)}[fmt]
    v = np.moveaxis(np.asarray(x, np.float32).astype(ml_dtypes.bfloat16).astype(np.float64), axis, -1)
    blocks = v.reshape(v.shape[:-1] + (-1, 32))
    amax = np.abs(blocks).max(-1, keepdims=True)
    byte = np.maximum(np.where(amax > 0, np.frexp(amax)[1] - 1 + 127, 0) - down, 1)
    scale = np.exp2(byte - 127.0)
    codes = (blocks / scale).astype(np.float32).astype(dtype).astype(np.float64)
    return np.moveaxis((codes * scale).reshape(v.shape), -1, axis)


WIDE = False


def mx_kscale(k):
    if not WIDE:
        return np.ones(k)
    levels = np.array([10, -10, 5, -5, 0])
    if k % 512:
        return np.exp2(np.random.permutation(np.resize(levels, k // 32))).repeat(32)
    a = np.empty((k // 512, 16))
    for p in range(k // 512):
        a[p, :8] = np.random.permutation(np.resize(levels, 8))
        for g in range(8):
            far = levels[np.abs(levels - a[p, g]) >= 10]
            a[p, g + 8] = far[np.random.randint(len(far))]
    return np.exp2(a.ravel()).repeat(32)


def f64(x):
    return np.asarray(x).astype(np.float64)


def striped8(idx):
    return np.concatenate([v.reshape(-1, 16).T for v in idx]).astype(np.uint16)


def unstriped8(offs):
    return np.stack([offs[16 * g:16 * g + 16].T.reshape(-1) for g in range(8)]).astype(np.int64)


E2M1 = np.array([0.0, 0.5, 1.0, 1.5, 2.0, 3.0, 4.0, 6.0, -0.0, -0.5, -1.0, -1.5, -2.0, -3.0, -4.0, -6.0])


def pack_weight(w, fmt):
    k, n = w.shape
    w = f64(np.asarray(w, np.float32).astype(ml_dtypes.bfloat16)).reshape(k // 32, 32, n)
    amax = np.abs(w).max(1)
    if fmt == "e4m3":
        byte = np.frexp(amax)[1] - 1 + 127 - 7
    else:
        mant, ex = np.frexp(amax / 6.0)
        byte = np.where(mant > 0.5, ex, ex - 1) + 127
    byte = np.clip(np.where(amax > 0, byte, 1), 1, 254)
    scaled = (w * np.exp2(127.0 - byte)[:, None, :]).reshape(k, n).astype(np.float32)
    by_word = np.ascontiguousarray(scaled.reshape(k // 512, 128, 4, n).transpose(0, 1, 3, 2))
    if fmt == "e4m3":
        words = by_word.astype(ml_dtypes.float8_e4m3fn).view(np.uint8)
    else:
        c = by_word.astype(ml_dtypes.float4_e2m1fn).view(np.uint8) & 0xF
        words = (c[..., 0::2] | (c[..., 1::2] << 4)).reshape(k // 512, 128, 2 * n)
    return np.ascontiguousarray(words), np.ascontiguousarray(byte.astype(np.uint8).reshape(k // 512, 16, n))


def unpack_weight(words, scales, fmt):
    g, _, n = scales.shape
    words = np.ascontiguousarray(words).reshape(g, 128, n, -1)
    if fmt == "e4m3":
        vals = words.view(ml_dtypes.float8_e4m3fn).astype(np.float64)
    else:
        nib = np.empty((g, 128, n, 4), np.uint8)
        nib[..., 0::2] = words & 0xF
        nib[..., 1::2] = words >> 4
        vals = E2M1[nib]
    vals = vals * np.repeat(np.exp2(scales.astype(np.float64) - 127.0), 8, axis=1)[..., None]
    return vals.transpose(0, 1, 3, 2).reshape(g * 512, n)


K, M, T, S = 1536, 128, 2048, 1024


def setup_inputs():
    n = np.random.standard_normal
    s = mx_kscale(K)[:, None]
    w = n((K, M)) / np.sqrt(K) / s
    p_w8 = pack_weight(w[:512], "e4m3")
    p_w4 = pack_weight(w[512:], "e2m1")
    return {
        "x": (n((K, S)) * s).astype(np.float32),
        "w8_words": p_w8[0],
        "w8_scales": p_w8[1],
        "w4_words": p_w4[0],
        "w4_scales": p_w4[1],
        "wgo": np.repeat(np.random.uniform(0.5, 2.0, (8, S)), 16, axis=0).astype(np.float32),
        "offs": striped8(np.stack([np.random.permutation(T)[:S] for _ in range(8)])),
    }


def reference(x, w8_words, w8_scales, w4_words, w4_scales, wgo, offs):
    x_ = mxq(f64(x), 0, "e4m3")
    w8_ = unpack_weight(w8_words, w8_scales, "e4m3")
    w4_ = unpack_weight(w4_words, w4_scales, "e2m1")
    y = w8_.T @ x_[:512] + w4_.T @ x_[512:]
    place = unstriped8(offs)[np.arange(M) % 128 // 16]
    out = np.zeros((M, T))
    out[np.arange(M)[:, None], place] = f64(wgo)[np.arange(M) % 128] * (y)
    return out

@@ -1,0 +1,108 @@
+from contextlib import ExitStack
+
+import concourse.mybir as mybir
+
+K, M, T, S = 1536, 128, 2048, 1024
+FLOPS = 2 * K * M * S
+
+F32 = mybir.dt.float32
+BF16 = mybir.dt.bfloat16
+I32 = mybir.dt.int32
+U32 = mybir.dt.uint32
+U16 = mybir.dt.uint16
+U8 = mybir.dt.uint8
+FP8X4 = mybir.dt.float8_e4m3fn_x4
+FP4X4 = mybir.dt.float4_e2m1fn_x4
+
+P = 128
+PACK = 4
+K_PASS = P * PACK
+PASSES = K // K_PASS
+N_FP4 = 128
+CHUNKS = [256, 256, 256, 128, 128]
+VECTOR_EIGHTHS = [[5, 5, 5], [0, 0, 4], [0, 0, 4], [0, 0, 0], [0, 0, 0]]
+
+
+def tile_list_hscat_o_none_kernel(tc, x, w8_words, w8_scales, w4_words, w4_scales, wgo, offs, out):
+    nc = tc.nc
+    starts = [sum(CHUNKS[:c]) for c in range(len(CHUNKS))]
+
+    with ExitStack() as ctx:
+        keep = ctx.enter_context(tc.tile_pool(name="keep", bufs=1))
+        psum = ctx.enter_context(tc.psum_pool(name="psum", bufs=1))
+
+        offsets = keep.tile([P, S // 16], U16, name="offsets")
+        window = keep.tile([P, T], F32, name="window")
+        w8 = keep.tile([P, PACK * M], U8, name="w8", align_bytes=64)
+        w4 = keep.tile([P, 2, 2 * M], U8, name="w4", align_bytes=64)
+        landed = keep.tile([P, PASSES * M], U8, name="landed", align_bytes=64)
+        planes = keep.tile([P, PASSES * M], U8, name="planes", align_bytes=64)
+        raw = [[keep.tile([P, PACK, w], F32, name="raw%d_%d" % (c, a)) for a in range(PASSES)] for c, w in enumerate(CHUNKS)]
+        gains = [keep.tile([P, w], F32, name="gain%d" % c) for c, w in enumerate(CHUNKS)]
+
+        def load_x(c, a):
+            rows = x[a * K_PASS : (a + 1) * K_PASS, starts[c] : starts[c] + CHUNKS[c]]
+            nc.sync.dma_start(out=raw[c][a][:], in_=rows.rearrange("(p j) w -> p j w", j=PACK))
+
+        def load_gain(c):
+            nc.sync.dma_start(out=gains[c][:], in_=wgo[:, starts[c] : starts[c] + CHUNKS[c]])
+
+        load_x(0, 0)
+        load_x(0, 1)
+        for q in range(4):
+            nc.sync.dma_start(out=landed[32 * q : 32 * q + 4, 0:M].bitcast(I32), in_=w8_scales[0, 4 * q : 4 * q + 4, :].bitcast(I32))
+        nc.sync.dma_start(out=w8[:].bitcast(I32), in_=w8_words[0].rearrange("p n t -> p (n t)").bitcast(I32))
+        load_x(0, 2)
+        load_x(1, 0)
+        for q in range(4):
+            nc.sync.dma_start(
+                out=landed[32 * q : 32 * q + 4, M:].rearrange("r (a n) -> r a n", a=2).bitcast(I32),
+                in_=w4_scales[:, 4 * q : 4 * q + 4, :].rearrange("a r n -> r a n").bitcast(I32),
+            )
+        nc.sync.dma_start(out=w4[:].bitcast(I32), in_=w4_words.rearrange("a p n -> p a n").bitcast(I32))
+        nc.sync.dma_start(offsets[:], offs)
+        load_x(1, 1)
+        load_gain(0)
+        load_x(1, 2)
+        load_gain(1)
+        for c in range(2, len(CHUNKS)):
+            for a in range(PASSES):
+                load_x(c, a)
+            load_gain(c)
+
+        nc.vector.memset(planes[:].bitcast(I32), 0)
+        nc.vector.memset(window[:], 0.0)
+        for q in range(4):
+            nc.vector.tensor_copy(out=planes[32 * q : 32 * q + 4, :].bitcast(I32), in_=landed[32 * q : 32 * q + 4, :].bitcast(I32))
+
+        for c, w in enumerate(CHUNKS):
+            acc = psum.tile([P, w], F32, name="acc%d" % c)
+            for a in range(PASSES):
+                grouped = keep.tile([P, w * PACK], BF16, name="grouped%d_%d" % (c, a), align_bytes=64)
+                codes = keep.tile([P, w], U32, name="codes%d_%d" % (c, a), align_bytes=64)
+                scales = keep.tile([P, w], U8, name="scales%d_%d" % (c, a), align_bytes=64)
+                cut = w * VECTOR_EIGHTHS[c][a] // 8
+                for lo, hi, copy in ((0, cut, nc.vector.tensor_copy), (cut, w, nc.scalar.copy)):
+                    if hi > lo:
+                        copy(
+                            out=grouped[:, lo * PACK : hi * PACK].rearrange("p (c i t) -> p c t i", i=4, t=PACK),
+                            in_=raw[c][a][:, :, lo:hi].rearrange("p t (c i) -> p c t i", i=4),
+                        )
+                nc.vector.quantize_mx(out=codes[:].bitcast(FP8X4), scales=scales[:], in_=grouped[:])
+                step = w if a == 0 else N_FP4
+                for n in range(0, w, step):
+                    nc.tensor.matmul_mx(
+                        out=acc[:, n : n + step],
+                        lhsT=w8[:].bitcast(FP8X4) if a == 0 else w4[:, a - 1, :].bitcast(FP4X4),
+                        lhsT_scale=planes[:, a * M : (a + 1) * M],
+                        rhs=codes[:, n : n + step].bitcast(FP8X4),
+                        rhs_scale=scales[:, n : n + step],
+                        start=(a == 0),
+                        stop=(a == PASSES - 1 and n + step == w),
+                    )
+            y = keep.tile([P, w], F32, name="y%d" % c)
+            nc.scalar.copy(out=y[:], in_=acc[:])
+            places = offsets[:, starts[c] // 16 : (starts[c] + w) // 16]
+            nc.vector.tensor_tensor(window[:].indirect(places), y[:], gains[c][:], mybir.AluOpType.mult)
+
+        nc.sync.dma_start(out=out, in_=window[:])

@@ -18,91 +18,113 @@ P = 128
 PACK = 4
 K_PASS = P * PACK
 PASSES = K // K_PASS
-N_FP4 = 128
-CHUNKS = [256, 256, 256, 128, 128]
-VECTOR_EIGHTHS = [[5, 5, 5], [0, 0, 4], [0, 0, 4], [0, 0, 0], [0, 0, 0]]
+LAST_PASS = PASSES - 1
+QUADRANTS = 4
+LIST_ROWS = 16
+UNIT = 128
+CHUNKS = [512, 256, 128, 128]
+PIECE = 256
+RUN = 4
 
 
 def tile_list_hscat_o_none_kernel(tc, x, w8_words, w8_scales, w4_words, w4_scales, wgo, offs, out):
     nc = tc.nc
     starts = [sum(CHUNKS[:c]) for c in range(len(CHUNKS))]
+    gain_spans = [(starts[0], CHUNKS[0]), (starts[1], CHUNKS[1]), (starts[2], S - starts[2])]
 
     with ExitStack() as ctx:
         keep = ctx.enter_context(tc.tile_pool(name="keep", bufs=1))
         psum = ctx.enter_context(tc.psum_pool(name="psum", bufs=1))
 
-        offsets = keep.tile([P, S // 16], U16, name="offsets")
+        offsets = keep.tile([P, S // LIST_ROWS], U16, name="offsets")
         window = keep.tile([P, T], F32, name="window")
         w8 = keep.tile([P, PACK * M], U8, name="w8", align_bytes=64)
-        w4 = keep.tile([P, 2, 2 * M], U8, name="w4", align_bytes=64)
-        landed = keep.tile([P, PASSES * M], U8, name="landed", align_bytes=64)
+        w4 = keep.tile([P, PASSES - 1, 2 * M], U8, name="w4", align_bytes=64)
+        w8_rows = keep.tile([P, M], U8, name="w8_rows", align_bytes=64)
         planes = keep.tile([P, PASSES * M], U8, name="planes", align_bytes=64)
+        gains = [keep.tile([P, w], F32, name="gain%d" % lo) for lo, w in gain_spans]
         raw = [[keep.tile([P, PACK, w], F32, name="raw%d_%d" % (c, a)) for a in range(PASSES)] for c, w in enumerate(CHUNKS)]
-        gains = [keep.tile([P, w], F32, name="gain%d" % c) for c, w in enumerate(CHUNKS)]
+        sums = [psum.tile([P, UNIT], F32, name="sum%d" % n) for n in range(0, S, UNIT)]
+
+        nc.vector.memset(planes[:].bitcast(I32), 0)
 
         def load_x(c, a):
             rows = x[a * K_PASS : (a + 1) * K_PASS, starts[c] : starts[c] + CHUNKS[c]]
-            nc.sync.dma_start(out=raw[c][a][:], in_=rows.rearrange("(p j) w -> p j w", j=PACK))
+            nc.sync.dma_start(out=raw[c][a][:], in_=rows.rearrange("(p t) w -> p t w", t=PACK))
 
-        def load_gain(c):
-            nc.sync.dma_start(out=gains[c][:], in_=wgo[:, starts[c] : starts[c] + CHUNKS[c]])
+        def load_gain(g):
+            lo, w = gain_spans[g]
+            nc.sync.dma_start(out=gains[g][:], in_=wgo[:, lo : lo + w])
 
         load_x(0, 0)
-        load_x(0, 1)
-        for q in range(4):
-            nc.sync.dma_start(out=landed[32 * q : 32 * q + 4, 0:M].bitcast(I32), in_=w8_scales[0, 4 * q : 4 * q + 4, :].bitcast(I32))
+        for q in range(QUADRANTS):
+            nc.sync.dma_start(out=w8_rows[32 * q : 32 * q + 4, :].bitcast(I32), in_=w8_scales[0, 4 * q : 4 * q + 4, :].bitcast(I32))
         nc.sync.dma_start(out=w8[:].bitcast(I32), in_=w8_words[0].rearrange("p n t -> p (n t)").bitcast(I32))
-        load_x(0, 2)
-        load_x(1, 0)
-        for q in range(4):
+        nc.sync.dma_start(out=w4[:].bitcast(I32), in_=w4_words.rearrange("a p n -> p a n").bitcast(I32))
+        load_x(0, 1)
+        for q in range(QUADRANTS):
             nc.sync.dma_start(
-                out=landed[32 * q : 32 * q + 4, M:].rearrange("r (a n) -> r a n", a=2).bitcast(I32),
+                out=planes[32 * q : 32 * q + 4, M:].rearrange("r (a n) -> r a n", a=PASSES - 1).bitcast(I32),
                 in_=w4_scales[:, 4 * q : 4 * q + 4, :].rearrange("a r n -> r a n").bitcast(I32),
             )
-        nc.sync.dma_start(out=w4[:].bitcast(I32), in_=w4_words.rearrange("a p n -> p a n").bitcast(I32))
+        load_x(0, LAST_PASS)
         nc.sync.dma_start(offsets[:], offs)
-        load_x(1, 1)
         load_gain(0)
-        load_x(1, 2)
-        load_gain(1)
-        for c in range(2, len(CHUNKS)):
+        for c in range(1, len(CHUNKS)):
             for a in range(PASSES):
                 load_x(c, a)
-            load_gain(c)
+            if c == 1 or c == len(CHUNKS) - 1:
+                load_gain(min(c, len(gain_spans) - 1))
 
-        nc.vector.memset(planes[:].bitcast(I32), 0)
         nc.vector.memset(window[:], 0.0)
-        for q in range(4):
-            nc.vector.tensor_copy(out=planes[32 * q : 32 * q + 4, :].bitcast(I32), in_=landed[32 * q : 32 * q + 4, :].bitcast(I32))
+        for q in range(QUADRANTS):
+            nc.vector.tensor_copy(out=planes[32 * q : 32 * q + 4, 0:M].bitcast(I32), in_=w8_rows[32 * q : 32 * q + 4, :].bitcast(I32))
 
-        for c, w in enumerate(CHUNKS):
-            acc = psum.tile([P, w], F32, name="acc%d" % c)
-            for a in range(PASSES):
-                grouped = keep.tile([P, w * PACK], BF16, name="grouped%d_%d" % (c, a), align_bytes=64)
-                codes = keep.tile([P, w], U32, name="codes%d_%d" % (c, a), align_bytes=64)
-                scales = keep.tile([P, w], U8, name="scales%d_%d" % (c, a), align_bytes=64)
-                cut = w * VECTOR_EIGHTHS[c][a] // 8
-                for lo, hi, copy in ((0, cut, nc.vector.tensor_copy), (cut, w, nc.scalar.copy)):
-                    if hi > lo:
-                        copy(
-                            out=grouped[:, lo * PACK : hi * PACK].rearrange("p (c i t) -> p c t i", i=4, t=PACK),
-                            in_=raw[c][a][:, :, lo:hi].rearrange("p t (c i) -> p c t i", i=4),
-                        )
-                nc.vector.quantize_mx(out=codes[:].bitcast(FP8X4), scales=scales[:], in_=grouped[:])
-                step = w if a == 0 else N_FP4
-                for n in range(0, w, step):
-                    nc.tensor.matmul_mx(
-                        out=acc[:, n : n + step],
-                        lhsT=w8[:].bitcast(FP8X4) if a == 0 else w4[:, a - 1, :].bitcast(FP4X4),
-                        lhsT_scale=planes[:, a * M : (a + 1) * M],
-                        rhs=codes[:, n : n + step].bitcast(FP8X4),
-                        rhs_scale=scales[:, n : n + step],
-                        start=(a == 0),
-                        stop=(a == PASSES - 1 and n + step == w),
+        def quantise(c, a, first, w):
+            name = "%d_%d" % (a, starts[c] + first)
+            grouped = keep.tile([P, w * PACK], BF16, name="grouped" + name, align_bytes=64)
+            codes = keep.tile([P, w], U32, name="codes" + name, align_bytes=64)
+            scales = keep.tile([P, w], U8, name="scales" + name, align_bytes=64)
+            cut = w // 2 if c == 0 or a == 0 else w
+            for lo, hi, copy in ((0, cut, nc.scalar.copy), (cut, w, nc.vector.tensor_copy)):
+                if hi > lo:
+                    copy(
+                        out=grouped[:, lo * PACK : hi * PACK].rearrange("p (r i t) -> p r t i", i=RUN, t=PACK),
+                        in_=raw[c][a][:, :, first + lo : first + hi].rearrange("p t (r i) -> p r t i", i=RUN),
                     )
-            y = keep.tile([P, w], F32, name="y%d" % c)
-            nc.scalar.copy(out=y[:], in_=acc[:])
-            places = offsets[:, starts[c] // 16 : (starts[c] + w) // 16]
-            nc.vector.tensor_tensor(window[:].indirect(places), y[:], gains[c][:], mybir.AluOpType.mult)
+            nc.vector.quantize_mx(out=codes[:].bitcast(FP8X4), scales=scales[:], in_=grouped[:])
+            return codes, scales
+
+        def multiply(n, a, codes, scales):
+            nc.tensor.matmul_mx(
+                out=sums[n // UNIT][:],
+                lhsT=w8[:].bitcast(FP8X4) if a == 0 else w4[:, a - 1, :].bitcast(FP4X4),
+                lhsT_scale=planes[:, a * M : (a + 1) * M],
+                rhs=codes.bitcast(FP8X4),
+                rhs_scale=scales,
+                start=(a == 0),
+                stop=(a == LAST_PASS),
+            )
+
+        def place(n, y):
+            g = max(i for i, (lo, w) in enumerate(gain_spans) if lo <= n)
+            gain = gains[g][:, n - gain_spans[g][0] : n - gain_spans[g][0] + UNIT]
+            nc.scalar.copy(out=y, in_=sums[n // UNIT][:])
+            places = offsets[:, n // LIST_ROWS : (n + UNIT) // LIST_ROWS]
+            nc.vector.tensor_tensor(window[:].indirect(places), y, gain, mybir.AluOpType.mult)
+
+        for c, width in enumerate(CHUNKS):
+            for a in range(PASSES):
+                w = UNIT if a == LAST_PASS else min(width, PIECE)
+                for first in range(0, width, w):
+                    codes, scales = quantise(c, a, first, w)
+                    for u in range(0, w, UNIT):
+                        multiply(starts[c] + first + u, a, codes[:, u : u + UNIT], scales[:, u : u + UNIT])
+                    if a == LAST_PASS and first == 0 and c > 0:
+                        place(starts[c] - UNIT, raw[c][a][:, 0, 0:UNIT])
+            for u in range(width // UNIT - 1):
+                place(starts[c] + u * UNIT, raw[c][LAST_PASS][:, u, width - UNIT :])
+        y_last = keep.tile([P, UNIT], F32, name="y_last")
+        place(S - UNIT, y_last[:])
 
         nc.sync.dma_start(out=out, in_=window[:])

from contextlib import ExitStack

import concourse.mybir as mybir

K, M, T, S = 1536, 128, 2048, 1024
FLOPS = 2 * K * M * S

F32 = mybir.dt.float32
BF16 = mybir.dt.bfloat16
I32 = mybir.dt.int32
U32 = mybir.dt.uint32
U16 = mybir.dt.uint16
U8 = mybir.dt.uint8
FP8X4 = mybir.dt.float8_e4m3fn_x4
FP4X4 = mybir.dt.float4_e2m1fn_x4

P = 128
PACK = 4
K_PASS = P * PACK
PASSES = K // K_PASS
LAST_PASS = PASSES - 1
QUADRANTS = 4
LIST_ROWS = 16
UNIT = 128
CHUNKS = [512, 256, 128, 128]
PIECE = 256
RUN = 4


def tile_list_hscat_o_none_kernel(tc, x, w8_words, w8_scales, w4_words, w4_scales, wgo, offs, out):
    nc = tc.nc
    starts = [sum(CHUNKS[:c]) for c in range(len(CHUNKS))]
    gain_spans = [(starts[0], CHUNKS[0]), (starts[1], CHUNKS[1]), (starts[2], S - starts[2])]

    with ExitStack() as ctx:
        keep = ctx.enter_context(tc.tile_pool(name="keep", bufs=1))
        psum = ctx.enter_context(tc.psum_pool(name="psum", bufs=1))

        offsets = keep.tile([P, S // LIST_ROWS], U16, name="offsets")
        window = keep.tile([P, T], F32, name="window")
        w8 = keep.tile([P, PACK * M], U8, name="w8", align_bytes=64)
        w4 = keep.tile([P, PASSES - 1, 2 * M], U8, name="w4", align_bytes=64)
        w8_rows = keep.tile([P, M], U8, name="w8_rows", align_bytes=64)
        planes = keep.tile([P, PASSES * M], U8, name="planes", align_bytes=64)
        gains = [keep.tile([P, w], F32, name="gain%d" % lo) for lo, w in gain_spans]
        raw = [[keep.tile([P, PACK, w], F32, name="raw%d_%d" % (c, a)) for a in range(PASSES)] for c, w in enumerate(CHUNKS)]
        sums = [psum.tile([P, UNIT], F32, name="sum%d" % n) for n in range(0, S, UNIT)]

        nc.vector.memset(planes[:].bitcast(I32), 0)

        def load_x(c, a):
            rows = x[a * K_PASS : (a + 1) * K_PASS, starts[c] : starts[c] + CHUNKS[c]]
            nc.sync.dma_start(out=raw[c][a][:], in_=rows.rearrange("(p t) w -> p t w", t=PACK))

        def load_gain(g):
            lo, w = gain_spans[g]
            nc.sync.dma_start(out=gains[g][:], in_=wgo[:, lo : lo + w])

        load_x(0, 0)
        for q in range(QUADRANTS):
            nc.sync.dma_start(out=w8_rows[32 * q : 32 * q + 4, :].bitcast(I32), in_=w8_scales[0, 4 * q : 4 * q + 4, :].bitcast(I32))
        nc.sync.dma_start(out=w8[:].bitcast(I32), in_=w8_words[0].rearrange("p n t -> p (n t)").bitcast(I32))
        nc.sync.dma_start(out=w4[:].bitcast(I32), in_=w4_words.rearrange("a p n -> p a n").bitcast(I32))
        load_x(0, 1)
        for q in range(QUADRANTS):
            nc.sync.dma_start(
                out=planes[32 * q : 32 * q + 4, M:].rearrange("r (a n) -> r a n", a=PASSES - 1).bitcast(I32),
                in_=w4_scales[:, 4 * q : 4 * q + 4, :].rearrange("a r n -> r a n").bitcast(I32),
            )
        load_x(0, LAST_PASS)
        nc.sync.dma_start(offsets[:], offs)
        load_gain(0)
        for c in range(1, len(CHUNKS)):
            for a in range(PASSES):
                load_x(c, a)
            if c == 1 or c == len(CHUNKS) - 1:
                load_gain(min(c, len(gain_spans) - 1))

        nc.vector.memset(window[:], 0.0)
        for q in range(QUADRANTS):
            nc.vector.tensor_copy(out=planes[32 * q : 32 * q + 4, 0:M].bitcast(I32), in_=w8_rows[32 * q : 32 * q + 4, :].bitcast(I32))

        def quantise(c, a, first, w):
            name = "%d_%d" % (a, starts[c] + first)
            grouped = keep.tile([P, w * PACK], BF16, name="grouped" + name, align_bytes=64)
            codes = keep.tile([P, w], U32, name="codes" + name, align_bytes=64)
            scales = keep.tile([P, w], U8, name="scales" + name, align_bytes=64)
            cut = w // 2 if c == 0 or a == 0 else w
            for lo, hi, copy in ((0, cut, nc.scalar.copy), (cut, w, nc.vector.tensor_copy)):
                if hi > lo:
                    copy(
                        out=grouped[:, lo * PACK : hi * PACK].rearrange("p (r i t) -> p r t i", i=RUN, t=PACK),
                        in_=raw[c][a][:, :, first + lo : first + hi].rearrange("p t (r i) -> p r t i", i=RUN),
                    )
            nc.vector.quantize_mx(out=codes[:].bitcast(FP8X4), scales=scales[:], in_=grouped[:])
            return codes, scales

        def multiply(n, a, codes, scales):
            nc.tensor.matmul_mx(
                out=sums[n // UNIT][:],
                lhsT=w8[:].bitcast(FP8X4) if a == 0 else w4[:, a - 1, :].bitcast(FP4X4),
                lhsT_scale=planes[:, a * M : (a + 1) * M],
                rhs=codes.bitcast(FP8X4),
                rhs_scale=scales,
                start=(a == 0),
                stop=(a == LAST_PASS),
            )

        def place(n, y):
            g = max(i for i, (lo, w) in enumerate(gain_spans) if lo <= n)
            gain = gains[g][:, n - gain_spans[g][0] : n - gain_spans[g][0] + UNIT]
            nc.scalar.copy(out=y, in_=sums[n // UNIT][:])
            places = offsets[:, n // LIST_ROWS : (n + UNIT) // LIST_ROWS]
            nc.vector.tensor_tensor(window[:].indirect(places), y, gain, mybir.AluOpType.mult)

        for c, width in enumerate(CHUNKS):
            for a in range(PASSES):
                w = UNIT if a == LAST_PASS else min(width, PIECE)
                for first in range(0, width, w):
                    codes, scales = quantise(c, a, first, w)
                    for u in range(0, w, UNIT):
                        multiply(starts[c] + first + u, a, codes[:, u : u + UNIT], scales[:, u : u + UNIT])
                    if a == LAST_PASS and first == 0 and c > 0:
                        place(starts[c] - UNIT, raw[c][a][:, 0, 0:UNIT])
            for u in range(width // UNIT - 1):
                place(starts[c] + u * UNIT, raw[c][LAST_PASS][:, u, width - UNIT :])
        y_last = keep.tile([P, UNIT], F32, name="y_last")
        place(S - UNIT, y_last[:])

        nc.sync.dma_start(out=out, in_=window[:])
